import numpy as np
import ml_dtypes


def mxq(x, axis, fmt="e4m3"):
    dtype, down = {"e4m3": (ml_dtypes.float8_e4m3fn, 7), "e5m2": (ml_dtypes.float8_e5m2, 14)}[fmt]
    v = np.moveaxis(np.asarray(x, np.float32).astype(ml_dtypes.bfloat16).astype(np.float64), axis, -1)
    blocks = v.reshape(v.shape[:-1] + (-1, 32))
    amax = np.abs(blocks).max(-1, keepdims=True)
    byte = np.maximum(np.where(amax > 0, np.frexp(amax)[1] - 1 + 127, 0) - down, 1)
    scale = np.exp2(byte - 127.0)
    codes = (blocks / scale).astype(np.float32).astype(dtype).astype(np.float64)
    return np.moveaxis((codes * scale).reshape(v.shape), -1, axis)


WIDE = False


def mx_kscale(k):
    if not WIDE:
        return np.ones(k)
    levels = np.array([10, -10, 5, -5, 0])
    if k % 512:
        return np.exp2(np.random.permutation(np.resize(levels, k // 32))).repeat(32)
    a = np.empty((k // 512, 16))
    for p in range(k // 512):
        a[p, :8] = np.random.permutation(np.resize(levels, 8))
        for g in range(8):
            far = levels[np.abs(levels - a[p, g]) >= 10]
            a[p, g + 8] = far[np.random.randint(len(far))]
    return np.exp2(a.ravel()).repeat(32)


def f64(x):
    return np.asarray(x).astype(np.float64)


def striped(idx):
    return np.tile(idx.reshape(-1, 16).T, (8, 1)).astype(np.uint16)


def unstriped(offs):
    return offs[:16].T.reshape(-1).astype(np.int64)


E2M1 = np.array([0.0, 0.5, 1.0, 1.5, 2.0, 3.0, 4.0, 6.0, -0.0, -0.5, -1.0, -1.5, -2.0, -3.0, -4.0, -6.0])


def pack_weight(w, fmt):
    k, n = w.shape
    w = f64(np.asarray(w, np.float32).astype(ml_dtypes.bfloat16)).reshape(k // 32, 32, n)
    amax = np.abs(w).max(1)
    if fmt == "e4m3":
        byte = np.frexp(amax)[1] - 1 + 127 - 7
    else:
        mant, ex = np.frexp(amax / 6.0)
        byte = np.where(mant > 0.5, ex, ex - 1) + 127
    byte = np.clip(np.where(amax > 0, byte, 1), 1, 254)
    scaled = (w * np.exp2(127.0 - byte)[:, None, :]).reshape(k, n).astype(np.float32)
    by_word = np.ascontiguousarray(scaled.reshape(k // 512, 128, 4, n).transpose(0, 1, 3, 2))
    if fmt == "e4m3":
        words = by_word.astype(ml_dtypes.float8_e4m3fn).view(np.uint8)
    else:
        c = by_word.astype(ml_dtypes.float4_e2m1fn).view(np.uint8) & 0xF
        words = (c[..., 0::2] | (c[..., 1::2] << 4)).reshape(k // 512, 128, 2 * n)
    return np.ascontiguousarray(words), np.ascontiguousarray(byte.astype(np.uint8).reshape(k // 512, 16, n))


def unpack_weight(words, scales, fmt):
    g, _, n = scales.shape
    words = np.ascontiguousarray(words).reshape(g, 128, n, -1)
    if fmt == "e4m3":
        vals = words.view(ml_dtypes.float8_e4m3fn).astype(np.float64)
    else:
        nib = np.empty((g, 128, n, 4), np.uint8)
        nib[..., 0::2] = words & 0xF
        nib[..., 1::2] = words >> 4
        vals = E2M1[nib]
    vals = vals * np.repeat(np.exp2(scales.astype(np.float64) - 127.0), 8, axis=1)[..., None]
    return vals.transpose(0, 1, 3, 2).reshape(g * 512, n)


def gelu(v):
    return 0.5 * v * (1.0 + np.tanh(np.sqrt(2.0 / np.pi) * (v + 0.044715 * v**3)))


K, T, S, H, T3, S2, P = 512, 4096, 1024, 1024, 2048, 512, 512

def setup_inputs():
    n = np.random.standard_normal
    s = mx_kscale(K)[:, None]
    u = mx_kscale(H)[:, None]
    d = {}
    d["tab_words"], d["tab_scales"] = pack_weight(n((K, T)) * s, "e4m3")
    d["tab2_words"], d["tab2_scales"] = pack_weight(n((H, T3)) / u / H ** 0.5, "e4m3")
    d["w1"] = (1.5 * n((K, H)) / s / K ** 0.5).astype(np.float32)
    d["w4_words"], d["w4_scales"] = pack_weight(1.5 * n((K, H)) / s / K ** 0.5, "e2m1")
    d["b1"] = (0.7 * n(H)).astype(np.float32)
    d["gain"] = (np.exp(0.3 * n(H)) * u[:, 0]).astype(np.float32)
    d["tension"] = (1.2 * n((S2, P))).astype(np.float32)
    d["offs"] = striped(np.random.permutation(T)[:S])
    d["offs2"] = striped(np.random.permutation(T3)[:S2])
    d["pos1"] = striped(np.random.permutation(S)[:P])
    d["pos2"] = striped(np.random.permutation(S)[:P])
    return d

def reference(tab_words, tab_scales, tab2_words, tab2_scales, w1, w4_words, w4_scales,
              b1, gain, tension, offs, offs2, pos1, pos2):
    v = unpack_weight(tab_words, tab_scales, "e4m3")[:, unstriped(offs)]
    v2 = unpack_weight(tab2_words, tab2_scales, "e4m3")[:, unstriped(offs2)]
    w4 = unpack_weight(w4_words, w4_scales, "e2m1")
    a = (mxq(f64(w1), 0, "e4m3").T @ v) + f64(b1)[:, None]
    b = w4.T @ v
    ga = 0.5 * a * (1.0 + np.tanh(0.7978845608028654 * (a + 0.044715 * a ** 3)))
    gb = 0.5 * b * (1.0 + np.tanh(0.7978845608028654 * (b + 0.044715 * b ** 3)))
    h = (ga - gb) * f64(gain)[:, None]
    e = v2.T @ mxq(h, 0, "e4m3")
    haul = e[:, unstriped(pos1)]
    track = e[:, unstriped(pos2)]
    return haul * (f64(tension) - track)

@@ -1,0 +1,232 @@
+from contextlib import ExitStack
+
+import concourse.mybir as mybir
+
+K, T, S, H, T3, S2, NP = 512, 4096, 1024, 1024, 2048, 512, 512
+FLOPS = 2 * (2 * K * H * S + H * S2 * S)
+
+F32 = mybir.dt.float32
+BF16 = mybir.dt.bfloat16
+I32 = mybir.dt.int32
+U32 = mybir.dt.uint32
+U16 = mybir.dt.uint16
+U8 = mybir.dt.uint8
+FP8X4 = mybir.dt.float8_e4m3fn_x4
+FP4X4 = mybir.dt.float4_e2m1fn_x4
+ALU = mybir.AluOpType
+ACT = mybir.ActivationFunctionType
+
+P = 128
+PACK = 4
+N = 512
+R_PASSES = H // 512
+HALVES = S // N
+M_TILES = S2 // P
+
+
+def tile_list_rope_window_scores_kernel(
+    tc, tab_words, tab_scales, tab2_words, tab2_scales, w1, w4_words, w4_scales,
+    b1, gain, tension, offs, offs2, pos1, pos2, out,
+):
+    nc = tc.nc
+    with ExitStack() as ctx:
+        keep = ctx.enter_context(tc.tile_pool(name="keep", bufs=1))
+        ring = ctx.enter_context(tc.tile_pool(name="ring", bufs=2))
+        acc_pool = ctx.enter_context(tc.psum_pool(name="acc", bufs=4))
+        e_pool = ctx.enter_context(tc.psum_pool(name="epsum", bufs=1))
+
+        def held(name, shape, dtype, tag=None):
+            return keep.tile(shape, dtype, name=name, tag=tag or name, align_bytes=64)
+
+        offs_sb = held("offs_sb", [P, S // 16], U16)
+        offs2_sb = held("offs2_sb", [P, S2 // 16], U16)
+        pos1_sb = held("pos1_sb", [P, NP // 16], U16)
+        pos2_sb = held("pos2_sb", [P, NP // 16], U16)
+
+        w4w_raw = held("w4w_raw", [P, 2 * H], U8, tag="stage_a")
+        w4s_raw = held("w4s_raw", [P, H], U8, tag="stage_b")
+        tabw = held("tabw", [P, T], I32, tag="table_words")
+        tabs = held("tabs", [P, T], U8, tag="table_scales")
+        b1_sb = held("b1_sb", [P, R_PASSES, PACK], F32)
+        gain_sb = held("gain_sb", [P, R_PASSES, PACK], F32)
+        warm = held("warm", [P, 2], F32)
+
+        nc.gpsimd.memset(w4s_raw[:].bitcast(I32), 0)
+        nc.vector.memset(tabs[:].bitcast(I32), 0)
+        nc.vector.memset(warm[:, 0:1], 0.0)
+        nc.scalar.activation(warm[:, 1:2], warm[:, 0:1], ACT.Gelu_apprx_tanh)
+
+        for tile, src in ((offs_sb, offs), (offs2_sb, offs2), (pos2_sb, pos2), (pos1_sb, pos1)):
+            nc.sync.dma_start(tile[:], src)
+        nc.sync.dma_start(w4w_raw[:].bitcast(I32), w4_words[0].bitcast(I32))
+        for q in range(4):
+            nc.gpsimd.dma_start(w4s_raw[32 * q : 32 * q + 4, :].bitcast(I32), w4_scales[0, 4 * q : 4 * q + 4, :].bitcast(I32))
+        nc.sync.dma_start(tabw[:], tab_words[0].rearrange("p t i -> p (t i)").bitcast(I32))
+        nc.sync.dma_start(b1_sb[:], b1.rearrange("(b p t) -> p b t", b=R_PASSES, t=PACK))
+        nc.sync.dma_start(gain_sb[:], gain.rearrange("(b p t) -> p b t", b=R_PASSES, t=PACK))
+        for q in range(4):
+            nc.sync.dma_start(tabs[32 * q : 32 * q + 4, :].bitcast(I32), tab_scales[0, 4 * q : 4 * q + 4, :].bitcast(I32))
+
+        w4w = held("w4w", [P, 2 * H], U8)
+        w4s = held("w4s", [P, H], U8)
+        nc.vector.tensor_copy(
+            w4w[:].bitcast(U16).rearrange("p (b t m) -> p b t m", b=R_PASSES, t=PACK),
+            w4w_raw[:].bitcast(U16).rearrange("p (b m t) -> p b t m", b=R_PASSES, t=PACK),
+        )
+        nc.vector.tensor_copy(
+            w4s[:].rearrange("p (b t m) -> p b t m", b=R_PASSES, t=PACK),
+            w4s_raw[:].rearrange("p (b m t) -> p b t m", b=R_PASSES, t=PACK),
+        )
+
+        w1_rows = w1.rearrange("(p j) c -> p j c", j=PACK)
+        w1_raw = [held("w1_raw%d" % b, [P, PACK, 512], F32, tag=("stage_a", "stage_b")[b]) for b in range(R_PASSES)]
+        for b in range(R_PASSES):
+            nc.sync.dma_start(w1_raw[b][:], w1_rows[:, :, 512 * b : 512 * (b + 1)])
+
+        vw = [held("vw%d" % u, [P, N], U32) for u in range(HALVES)]
+        vs = [held("vs%d" % u, [P, N], U8) for u in range(HALVES)]
+
+        def gather_v(u):
+            cols = offs_sb[:, u * N // 16 : (u + 1) * N // 16]
+            nc.vector.tensor_copy(vw[u][:], tabw[:].bitcast(U32).indirect(cols))
+            nc.vector.tensor_copy(vs[u][:], tabs[:].indirect(cols))
+
+        w1g = [held("w1g%d" % b, [P, 512 * PACK], BF16) for b in range(R_PASSES)]
+        w1w = [held("w1w%d" % b, [P, 512], U32) for b in range(R_PASSES)]
+        w1s = [held("w1s%d" % b, [P, 512], U8) for b in range(R_PASSES)]
+
+        def weave_w1(b):
+            nc.vector.tensor_copy(
+                w1g[b][:].rearrange("p (t m j) -> p m j t", t=PACK, j=PACK),
+                w1_raw[b][:].rearrange("p j (m t) -> p m j t", t=PACK),
+            )
+
+        def quant_w1(b):
+            nc.vector.quantize_mx(out=w1w[b][:].bitcast(FP8X4), scales=w1s[b][:], in_=w1g[b][:])
+
+        v2w = [held("v2w%d" % a, [P, S2], U32) for a in range(R_PASSES)]
+        v2s = held("v2s", [P, S2], U8)
+
+        def gather_v2():
+            tab2w = held("tab2w", [P, R_PASSES * T3], I32, tag="table_words")
+            tab2s = held("tab2s", [P, T3], U8, tag="table_scales")
+            for a in range(R_PASSES):
+                nc.sync.dma_start(tab2w[:, T3 * a : T3 * (a + 1)], tab2_words[a].rearrange("p t i -> p (t i)").bitcast(I32))
+            nc.gpsimd.memset(tab2s[:].bitcast(I32), 0)
+            for q in range(4):
+                nc.sync.dma_start(tab2s[32 * q : 32 * q + 8, :].bitcast(I32), tab2_scales[:, 4 * q : 4 * q + 4, :].bitcast(I32))
+            nc.vector.tensor_copy(v2s[:], tab2s[:].indirect(offs2_sb[:]))
+            for a in range(R_PASSES):
+                nc.vector.tensor_copy(v2w[a][:], tab2w[:, T3 * a : T3 * (a + 1)].bitcast(U32).indirect(offs2_sb[:]))
+
+        chunks = [(u, b) for u in range(HALVES) for b in range(R_PASSES)]
+        hw = [held("hw%d" % c, [P, N], U32) for c in range(len(chunks))]
+        hs = [held("hs%d" % c, [P, N], U8) for c in range(len(chunks))]
+        scores = [held("scores%d" % m, [P, S], F32) for m in range(M_TILES)]
+        ga, gb, diff, hb, e_acc = {}, {}, {}, {}, {}
+
+        def read_b(c):
+            u, b = chunks[c]
+            gb[c] = ring.tile([P, PACK, N], F32, name="gb")
+            for t in range(PACK):
+                col = 512 * b + P * t
+                acc = acc_pool.tile([P, N], F32, name="acc")
+                nc.tensor.matmul_mx(
+                    out=acc[:], lhsT=w4w[:, 2 * col : 2 * (col + P)].bitcast(FP4X4), lhsT_scale=w4s[:, col : col + P],
+                    rhs=vw[u][:].bitcast(FP8X4), rhs_scale=vs[u][:], start=True, stop=True,
+                )
+                nc.scalar.activation(gb[c][:, t, :], acc[:], ACT.Gelu_apprx_tanh)
+
+        def read_a(c):
+            u, b = chunks[c]
+            ga[c] = ring.tile([P, PACK, N], F32, name="ga")
+            for t in range(PACK):
+                acc = acc_pool.tile([P, N], F32, name="acc")
+                nc.tensor.matmul_mx(
+                    out=acc[:], lhsT=w1w[b][:, P * t : P * (t + 1)].bitcast(FP8X4), lhsT_scale=w1s[b][:, P * t : P * (t + 1)],
+                    rhs=vw[u][:].bitcast(FP8X4), rhs_scale=vs[u][:], start=True, stop=True,
+                )
+                nc.scalar.activation(ga[c][:, t, :], acc[:], ACT.Gelu_apprx_tanh, bias=b1_sb[:, b, t : t + 1])
+
+        def subtract(c):
+            diff[c] = ring.tile([P, PACK, N], F32, name="diff")
+            for t0 in (0, 2):
+                nc.vector.tensor_tensor(diff[c][:, t0 : t0 + 2, :], ga[c][:, t0 : t0 + 2, :], gb[c][:, t0 : t0 + 2, :], ALU.subtract)
+
+        def scale_weave(c, j0, j1):
+            u, b = chunks[c]
+            if j0 == 0:
+                hb[c] = ring.tile([P, N * PACK], BF16, name="hb", align_bytes=64)
+            groups = (j1 - j0) // 4
+            nc.vector.tensor_tensor(
+                hb[c][:, PACK * j0 : PACK * j1].rearrange("p (g i t) -> p g t i", i=4, t=PACK),
+                diff[c][:, :, j0:j1].rearrange("p t (g i) -> p g t i", i=4),
+                gain_sb[:, b, :].rearrange("p (g t i) -> p g t i", g=1, i=1).to_broadcast([P, groups, PACK, 4]),
+                ALU.mult,
+            )
+
+        def quant_h(c, j0, j1):
+            nc.vector.quantize_mx(out=hw[c][:, j0:j1].bitcast(FP8X4), scales=hs[c][:, j0:j1], in_=hb[c][:, PACK * j0 : PACK * j1])
+
+        def score(c):
+            u, b = chunks[c]
+            for m in range(M_TILES):
+                if b == 0:
+                    e_acc[m] = e_pool.tile([P, N], F32, name="e%d" % m)
+                nc.tensor.matmul_mx(
+                    out=e_acc[m][:], lhsT=v2w[b][:, P * m : P * (m + 1)].bitcast(FP8X4), lhsT_scale=v2s[4 * b : P, P * m : P * (m + 1)],
+                    rhs=hw[c][:].bitcast(FP8X4), rhs_scale=hs[c][:], start=(b == 0), stop=(b == R_PASSES - 1),
+                )
+                if b == R_PASSES - 1:
+                    nc.scalar.copy(scores[m][:, N * u : N * (u + 1)], e_acc[m][:])
+
+        gather_v(0)
+        read_b(0)
+        weave_w1(0)
+        gather_v(1)
+        quant_w1(0)
+        read_a(0)
+        weave_w1(1)
+        read_b(1)
+        subtract(0)
+        quant_w1(1)
+        read_a(1)
+        scale_weave(0, 0, N)
+        last = len(chunks) - 1
+        for c in range(1, len(chunks)):
+            if c + 1 <= last:
+                read_b(c + 1)
+                read_a(c + 1)
+            subtract(c)
+            quant_h(c - 1, 0, N)
+            if c == 1:
+                gather_v2()
+            score(c - 1)
+            if c < last:
+                scale_weave(c, 0, N)
+        scale_weave(last, 0, N // 2)
+        scale_weave(last, N // 2, N)
+        quant_h(last, 0, N // 2)
+        quant_h(last, N // 2, N)
+        score(last)
+
+        tens = held("tens", [P, M_TILES, NP], F32, tag="stage_a")
+        nc.sync.dma_start(tens[:], tension.rearrange("(m p) j -> p m j", p=P))
+        above, left = {}, {}
+
+        def track(m):
+            above[m] = ring.tile([P, NP], F32, name="above")
+            left[m] = ring.tile([P, NP], F32, name="left")
+            nc.vector.tensor_tensor(above[m][:], scores[m][:].indirect(pos2_sb[:]), tens[:, m, :], ALU.subtract)
+            nc.scalar.mul(left[m][:], above[m][:], -1.0)
+
+        def haul(m):
+            res = ring.tile([P, NP], F32, name="res")
+            nc.vector.tensor_tensor(res[:], scores[m][:].indirect(pos1_sb[:]), left[m][:], ALU.mult)
+            nc.sync.dma_start(out[P * m : P * (m + 1), :], res[:])
+
+        track(0)
+        for m in range(M_TILES):
+            if m + 1 < M_TILES:
+                track(m + 1)
+            haul(m)

@@ -46,26 +46,18 @@ def tile_list_rope_window_scores_kernel(
         w4w_raw = held("w4w_raw", [P, 2 * H], U8, tag="stage_a")
         w4s_raw = held("w4s_raw", [P, H], U8, tag="stage_b")
         tabw = held("tabw", [P, T], I32, tag="table_words")
-        tabs = held("tabs", [P, T], U8, tag="table_scales")
-        b1_sb = held("b1_sb", [P, R_PASSES, PACK], F32)
-        gain_sb = held("gain_sb", [P, R_PASSES, PACK], F32)
-        warm = held("warm", [P, 2], F32)
+        tabs = held("tabs", [P, T], U8, tag="stage_c")
 
-        nc.gpsimd.memset(w4s_raw[:].bitcast(I32), 0)
         nc.vector.memset(tabs[:].bitcast(I32), 0)
-        nc.vector.memset(warm[:, 0:1], 0.0)
-        nc.scalar.activation(warm[:, 1:2], warm[:, 0:1], ACT.Gelu_apprx_tanh)
+        nc.gpsimd.memset(w4s_raw[:].bitcast(I32), 0)
 
         for tile, src in ((offs_sb, offs), (offs2_sb, offs2), (pos2_sb, pos2), (pos1_sb, pos1)):
             nc.sync.dma_start(tile[:], src)
         nc.sync.dma_start(w4w_raw[:].bitcast(I32), w4_words[0].bitcast(I32))
-        for q in range(4):
-            nc.gpsimd.dma_start(w4s_raw[32 * q : 32 * q + 4, :].bitcast(I32), w4_scales[0, 4 * q : 4 * q + 4, :].bitcast(I32))
         nc.sync.dma_start(tabw[:], tab_words[0].rearrange("p t i -> p (t i)").bitcast(I32))
-        nc.sync.dma_start(b1_sb[:], b1.rearrange("(b p t) -> p b t", b=R_PASSES, t=PACK))
-        nc.sync.dma_start(gain_sb[:], gain.rearrange("(b p t) -> p b t", b=R_PASSES, t=PACK))
+        nc.scalar.dma_start(tabs[0:P:8, :].bitcast(I32), tab_scales[0].bitcast(I32))
         for q in range(4):
-            nc.sync.dma_start(tabs[32 * q : 32 * q + 4, :].bitcast(I32), tab_scales[0, 4 * q : 4 * q + 4, :].bitcast(I32))
+            nc.scalar.dma_start(w4s_raw[32 * q : 32 * q + 4, :].bitcast(I32), w4_scales[0, 4 * q : 4 * q + 4, :].bitcast(I32))
 
         w4w = held("w4w", [P, 2 * H], U8)
         w4s = held("w4s", [P, H], U8)
@@ -73,6 +65,8 @@ def tile_list_rope_window_scores_kernel(
             w4w[:].bitcast(U16).rearrange("p (b t m) -> p b t m", b=R_PASSES, t=PACK),
             w4w_raw[:].bitcast(U16).rearrange("p (b m t) -> p b t m", b=R_PASSES, t=PACK),
         )
+        vs_spread = held("vs_spread", [P, S], U8, tag="stage_d")
+        nc.vector.tensor_copy(vs_spread[:], tabs[:].indirect(offs_sb[:]))
         nc.vector.tensor_copy(
             w4s[:].rearrange("p (b t m) -> p b t m", b=R_PASSES, t=PACK),
             w4s_raw[:].rearrange("p (b m t) -> p b t m", b=R_PASSES, t=PACK),
@@ -80,16 +74,21 @@ def tile_list_rope_window_scores_kernel(
 
         w1_rows = w1.rearrange("(p j) c -> p j c", j=PACK)
         w1_raw = [held("w1_raw%d" % b, [P, PACK, 512], F32, tag=("stage_a", "stage_b")[b]) for b in range(R_PASSES)]
-        for b in range(R_PASSES):
-            nc.sync.dma_start(w1_raw[b][:], w1_rows[:, :, 512 * b : 512 * (b + 1)])
+        nc.sync.dma_start(w1_raw[0][:], w1_rows[:, :, 0:512])
+        vs = held("vs", [P, S], U8)
+        for q in range(4):
+            nc.scalar.dma_start(vs[32 * q : 32 * q + 4, :].bitcast(I32), vs_spread[32 * q : 32 * (q + 1) : 8, :].bitcast(I32))
+        nc.sync.dma_start(w1_raw[1][:], w1_rows[:, :, 512:1024])
+        rows = held("rows", [P, 2, R_PASSES, PACK], F32, tag="stage_c")
+        b1_sb, gain_sb = rows[:, 0, :, :], rows[:, 1, :, :]
+        nc.sync.dma_start(b1_sb, b1.rearrange("(b p t) -> p b t", b=R_PASSES, t=PACK))
+        nc.sync.dma_start(gain_sb, gain.rearrange("(b p t) -> p b t", b=R_PASSES, t=PACK))
 
         vw = [held("vw%d" % u, [P, N], U32) for u in range(HALVES)]
-        vs = [held("vs%d" % u, [P, N], U8) for u in range(HALVES)]
 
         def gather_v(u):
             cols = offs_sb[:, u * N // 16 : (u + 1) * N // 16]
             nc.vector.tensor_copy(vw[u][:], tabw[:].bitcast(U32).indirect(cols))
-            nc.vector.tensor_copy(vs[u][:], tabs[:].indirect(cols))
 
         w1g = [held("w1g%d" % b, [P, 512 * PACK], BF16) for b in range(R_PASSES)]
         w1w = [held("w1w%d" % b, [P, 512], U32) for b in range(R_PASSES)]
@@ -109,7 +108,7 @@ def tile_list_rope_window_scores_kernel(
 
         def gather_v2():
             tab2w = held("tab2w", [P, R_PASSES * T3], I32, tag="table_words")
-            tab2s = held("tab2s", [P, T3], U8, tag="table_scales")
+            tab2s = held("tab2s", [P, T3], U8, tag="stage_d")
             for a in range(R_PASSES):
                 nc.sync.dma_start(tab2w[:, T3 * a : T3 * (a + 1)], tab2_words[a].rearrange("p t i -> p (t i)").bitcast(I32))
             nc.gpsimd.memset(tab2s[:].bitcast(I32), 0)
@@ -133,7 +132,7 @@ def tile_list_rope_window_scores_kernel(
                 acc = acc_pool.tile([P, N], F32, name="acc")
                 nc.tensor.matmul_mx(
                     out=acc[:], lhsT=w4w[:, 2 * col : 2 * (col + P)].bitcast(FP4X4), lhsT_scale=w4s[:, col : col + P],
-                    rhs=vw[u][:].bitcast(FP8X4), rhs_scale=vs[u][:], start=True, stop=True,
+                    rhs=vw[u][:].bitcast(FP8X4), rhs_scale=vs[:, N * u : N * (u + 1)], start=True, stop=True,
                 )
                 nc.scalar.activation(gb[c][:, t, :], acc[:], ACT.Gelu_apprx_tanh)
 
@@ -144,7 +143,7 @@ def tile_list_rope_window_scores_kernel(
                 acc = acc_pool.tile([P, N], F32, name="acc")
                 nc.tensor.matmul_mx(
                     out=acc[:], lhsT=w1w[b][:, P * t : P * (t + 1)].bitcast(FP8X4), lhsT_scale=w1s[b][:, P * t : P * (t + 1)],
-                    rhs=vw[u][:].bitcast(FP8X4), rhs_scale=vs[u][:], start=True, stop=True,
+                    rhs=vw[u][:].bitcast(FP8X4), rhs_scale=vs[:, N * u : N * (u + 1)], start=True, stop=True,
                 )
                 nc.scalar.activation(ga[c][:, t, :], acc[:], ACT.Gelu_apprx_tanh, bias=b1_sb[:, b, t : t + 1])
 
@@ -157,11 +156,11 @@ def tile_list_rope_window_scores_kernel(
             u, b = chunks[c]
             if j0 == 0:
                 hb[c] = ring.tile([P, N * PACK], BF16, name="hb", align_bytes=64)
-            groups = (j1 - j0) // 4
+            groups = (j1 - j0) // 2
             nc.vector.tensor_tensor(
-                hb[c][:, PACK * j0 : PACK * j1].rearrange("p (g i t) -> p g t i", i=4, t=PACK),
-                diff[c][:, :, j0:j1].rearrange("p t (g i) -> p g t i", i=4),
-                gain_sb[:, b, :].rearrange("p (g t i) -> p g t i", g=1, i=1).to_broadcast([P, groups, PACK, 4]),
+                hb[c][:, PACK * j0 : PACK * j1].rearrange("p (g i t) -> p g t i", i=2, t=PACK),
+                diff[c][:, :, j0:j1].rearrange("p t (g i) -> p g t i", i=2),
+                gain_sb[:, b, :].rearrange("p (g t i) -> p g t i", g=1, i=1).to_broadcast([P, groups, PACK, 2]),
                 ALU.mult,
             )
 

@@ -1,6 +1,7 @@
 from contextlib import ExitStack
 
 import concourse.mybir as mybir
+from concourse.masks import make_identity
 
 K, T, S, H, T3, S2, NP = 512, 4096, 1024, 1024, 2048, 512, 512
 FLOPS = 2 * (2 * K * H * S + H * S2 * S)
@@ -22,6 +23,8 @@ N = 512
 R_PASSES = H // 512
 HALVES = S // N
 M_TILES = S2 // P
+GPSIMD_SLICES = 2
+RING_BANKS = 7
 
 
 def tile_list_rope_window_scores_kernel(
@@ -32,8 +35,12 @@ def tile_list_rope_window_scores_kernel(
     with ExitStack() as ctx:
         keep = ctx.enter_context(tc.tile_pool(name="keep", bufs=1))
         ring = ctx.enter_context(tc.tile_pool(name="ring", bufs=2))
-        acc_pool = ctx.enter_context(tc.psum_pool(name="acc", bufs=4))
-        e_pool = ctx.enter_context(tc.psum_pool(name="epsum", bufs=1))
+        psum = ctx.enter_context(tc.psum_pool(name="psum", bufs=1))
+        taken = []
+
+        def next_bank():
+            taken.append(len(taken) % RING_BANKS)
+            return psum.tile([P, N], F32, name="bank%d" % taken[-1])
 
         def held(name, shape, dtype, tag=None):
             return keep.tile(shape, dtype, name=name, tag=tag or name, align_bytes=64)
@@ -79,10 +86,12 @@ def tile_list_rope_window_scores_kernel(
         for q in range(4):
             nc.scalar.dma_start(vs[32 * q : 32 * q + 4, :].bitcast(I32), vs_spread[32 * q : 32 * (q + 1) : 8, :].bitcast(I32))
         nc.sync.dma_start(w1_raw[1][:], w1_rows[:, :, 512:1024])
-        rows = held("rows", [P, 2, R_PASSES, PACK], F32, tag="stage_c")
-        b1_sb, gain_sb = rows[:, 0, :, :], rows[:, 1, :, :]
-        nc.sync.dma_start(b1_sb, b1.rearrange("(b p t) -> p b t", b=R_PASSES, t=PACK))
-        nc.sync.dma_start(gain_sb, gain.rearrange("(b p t) -> p b t", b=R_PASSES, t=PACK))
+        rows = held("rows", [P, 512], F32, tag="stage_c")
+        nc.gpsimd.memset(rows[:], 0.0)
+        nc.scalar.dma_start(rows[0:R_PASSES, :], b1.rearrange("(b c) -> b c", b=R_PASSES))
+        nc.scalar.dma_start(rows[R_PASSES : 2 * R_PASSES, :], gain.rearrange("(b c) -> b c", b=R_PASSES))
+        ident = held("ident", [P, P], F32)
+        make_identity(nc, ident[:])
 
         vw = [held("vw%d" % u, [P, N], U32) for u in range(HALVES)]
 
@@ -124,33 +133,44 @@ def tile_list_rope_window_scores_kernel(
         scores = [held("scores%d" % m, [P, S], F32) for m in range(M_TILES)]
         ga, gb, diff, hb, e_acc = {}, {}, {}, {}, {}
 
-        def read_b(c):
+        def read_b(c, t):
             u, b = chunks[c]
-            gb[c] = ring.tile([P, PACK, N], F32, name="gb")
-            for t in range(PACK):
-                col = 512 * b + P * t
-                acc = acc_pool.tile([P, N], F32, name="acc")
-                nc.tensor.matmul_mx(
-                    out=acc[:], lhsT=w4w[:, 2 * col : 2 * (col + P)].bitcast(FP4X4), lhsT_scale=w4s[:, col : col + P],
-                    rhs=vw[u][:].bitcast(FP8X4), rhs_scale=vs[:, N * u : N * (u + 1)], start=True, stop=True,
-                )
-                nc.scalar.activation(gb[c][:, t, :], acc[:], ACT.Gelu_apprx_tanh)
+            if t == 0:
+                gb[c] = ring.tile([P, PACK, N], F32, name="gb", bufs=3)
+            col = 512 * b + P * t
+            acc = next_bank()
+            nc.tensor.matmul_mx(
+                out=acc[:], lhsT=w4w[:, 2 * col : 2 * (col + P)].bitcast(FP4X4), lhsT_scale=w4s[:, col : col + P],
+                rhs=vw[u][:].bitcast(FP8X4), rhs_scale=vs[:, N * u : N * (u + 1)], start=True, stop=True,
+            )
+            nc.scalar.activation(gb[c][:, t, :], acc[:], ACT.Gelu_apprx_tanh)
 
-        def read_a(c):
+        def read_a(c, t):
             u, b = chunks[c]
-            ga[c] = ring.tile([P, PACK, N], F32, name="ga")
+            if t == 0:
+                ga[c] = ring.tile([P, PACK, N], F32, name="ga", bufs=3)
+            acc = next_bank()
+            nc.tensor.matmul_mx(
+                out=acc[:], lhsT=w1w[b][:, P * t : P * (t + 1)].bitcast(FP8X4), lhsT_scale=w1s[b][:, P * t : P * (t + 1)],
+                rhs=vw[u][:].bitcast(FP8X4), rhs_scale=vs[:, N * u : N * (u + 1)], start=True, stop=True,
+            )
+            nc.scalar.activation(ga[c][:, t, :], acc[:], ACT.Gelu_apprx_tanh, bias=b1_sb[:, t, b : b + 1])
+
+        def read_both(c):
             for t in range(PACK):
-                acc = acc_pool.tile([P, N], F32, name="acc")
-                nc.tensor.matmul_mx(
-                    out=acc[:], lhsT=w1w[b][:, P * t : P * (t + 1)].bitcast(FP8X4), lhsT_scale=w1s[b][:, P * t : P * (t + 1)],
-                    rhs=vw[u][:].bitcast(FP8X4), rhs_scale=vs[:, N * u : N * (u + 1)], start=True, stop=True,
-                )
-                nc.scalar.activation(ga[c][:, t, :], acc[:], ACT.Gelu_apprx_tanh, bias=b1_sb[:, b, t : t + 1])
+                read_b(c, t)
+                read_a(c, t)
 
         def subtract(c):
-            diff[c] = ring.tile([P, PACK, N], F32, name="diff")
-            for t0 in (0, 2):
-                nc.vector.tensor_tensor(diff[c][:, t0 : t0 + 2, :], ga[c][:, t0 : t0 + 2, :], gb[c][:, t0 : t0 + 2, :], ALU.subtract)
+            diff[c] = ring.tile([P, PACK, N], F32, name="diff", bufs=3)
+            for t in range(GPSIMD_SLICES):
+                nc.gpsimd.tensor_tensor(diff[c][:, t, :], ga[c][:, t, :], gb[c][:, t, :], ALU.subtract)
+            if c < len(chunks) - 1:
+                rest = [slice(GPSIMD_SLICES, PACK)]
+            else:
+                rest = [slice(t, t + 1) for t in range(GPSIMD_SLICES, PACK)]
+            for ts in rest:
+                nc.vector.tensor_tensor(diff[c][:, ts, :], ga[c][:, ts, :], gb[c][:, ts, :], ALU.subtract)
 
         def scale_weave(c, j0, j1):
             u, b = chunks[c]
@@ -160,54 +180,68 @@ def tile_list_rope_window_scores_kernel(
             nc.vector.tensor_tensor(
                 hb[c][:, PACK * j0 : PACK * j1].rearrange("p (g i t) -> p g t i", i=2, t=PACK),
                 diff[c][:, :, j0:j1].rearrange("p t (g i) -> p g t i", i=2),
-                gain_sb[:, b, :].rearrange("p (g t i) -> p g t i", g=1, i=1).to_broadcast([P, groups, PACK, 2]),
+                turned[:, :, R_PASSES + b : R_PASSES + b + 1].rearrange("p (g t) i -> p g t i", g=1).to_broadcast([P, groups, PACK, 2]),
                 ALU.mult,
             )
 
         def quant_h(c, j0, j1):
             nc.vector.quantize_mx(out=hw[c][:, j0:j1].bitcast(FP8X4), scales=hs[c][:, j0:j1], in_=hb[c][:, PACK * j0 : PACK * j1])
 
-        def score(c):
+        def score(c, m):
             u, b = chunks[c]
-            for m in range(M_TILES):
-                if b == 0:
-                    e_acc[m] = e_pool.tile([P, N], F32, name="e%d" % m)
-                nc.tensor.matmul_mx(
-                    out=e_acc[m][:], lhsT=v2w[b][:, P * m : P * (m + 1)].bitcast(FP8X4), lhsT_scale=v2s[4 * b : P, P * m : P * (m + 1)],
-                    rhs=hw[c][:].bitcast(FP8X4), rhs_scale=hs[c][:], start=(b == 0), stop=(b == R_PASSES - 1),
-                )
-                if b == R_PASSES - 1:
-                    nc.scalar.copy(scores[m][:, N * u : N * (u + 1)], e_acc[m][:])
+            if b == 0:
+                e_acc[m] = next_bank()
+            nc.tensor.matmul_mx(
+                out=e_acc[m][:], lhsT=v2w[b][:, P * m : P * (m + 1)].bitcast(FP8X4), lhsT_scale=v2s[4 * b : P, P * m : P * (m + 1)],
+                rhs=hw[c][:].bitcast(FP8X4), rhs_scale=hs[c][:], start=(b == 0), stop=(b == R_PASSES - 1),
+            )
+            if b == R_PASSES - 1:
+                nc.scalar.copy(scores[m][:, N * u : N * (u + 1)], e_acc[m][:])
 
         gather_v(0)
-        read_b(0)
-        weave_w1(0)
+        for t in range(PACK):
+            read_b(0, t)
+        for t in range(PACK // 2):
+            read_b(1, t)
+        turned = psum.tile([P, PACK, P], F32, name="turned")
+        for t in range(PACK):
+            nc.tensor.transpose(turned[:, t, :], rows[:, t:512:PACK], ident[:])
+        b1_sb = held("b1_sb", [P, PACK, R_PASSES], F32)
+        nc.scalar.copy(b1_sb[:], turned[:, :, 0:R_PASSES])
         gather_v(1)
+        weave_w1(0)
         quant_w1(0)
-        read_a(0)
+        for t in range(PACK):
+            read_a(0, t)
+        for t in range(PACK // 2, PACK):
+            read_b(1, t)
         weave_w1(1)
-        read_b(1)
-        subtract(0)
         quant_w1(1)
-        read_a(1)
+        for t in range(PACK):
+            read_a(1, t)
+        subtract(0)
         scale_weave(0, 0, N)
         last = len(chunks) - 1
         for c in range(1, len(chunks)):
             if c + 1 <= last:
-                read_b(c + 1)
-                read_a(c + 1)
+                read_both(c + 1)
             subtract(c)
             quant_h(c - 1, 0, N)
             if c == 1:
                 gather_v2()
-            score(c - 1)
             if c < last:
                 scale_weave(c, 0, N)
+        for m in range(M_TILES):
+            score(0, m)
+            score(1, m)
+        for m in range(M_TILES):
+            score(2, m)
         scale_weave(last, 0, N // 2)
         scale_weave(last, N // 2, N)
         quant_h(last, 0, N // 2)
         quant_h(last, N // 2, N)
-        score(last)
+        for m in range(M_TILES):
+            score(last, m)
 
         tens = held("tens", [P, M_TILES, NP], F32, tag="stage_a")
         nc.sync.dma_start(tens[:], tension.rearrange("(m p) j -> p m j", p=P))
@@ -221,8 +255,11 @@ def tile_list_rope_window_scores_kernel(
 
         def haul(m):
             res = ring.tile([P, NP], F32, name="res")
-            nc.vector.tensor_tensor(res[:], scores[m][:].indirect(pos1_sb[:]), left[m][:], ALU.mult)
-            nc.sync.dma_start(out[P * m : P * (m + 1), :], res[:])
+            width = NP if m < M_TILES - 1 else NP // 2
+            for j in range(0, NP, width):
+                picks = pos1_sb[:, j // 16 : (j + width) // 16]
+                nc.vector.tensor_tensor(res[:, j : j + width], scores[m][:].indirect(picks), left[m][:, j : j + width], ALU.mult)
+                nc.sync.dma_start(out[P * m : P * (m + 1), j : j + width], res[:, j : j + width])
 
         track(0)
         for m in range(M_TILES):

from contextlib import ExitStack

import concourse.mybir as mybir
from concourse.masks import make_identity

K, T, S, H, T3, S2, NP = 512, 4096, 1024, 1024, 2048, 512, 512
FLOPS = 2 * (2 * K * H * S + H * S2 * S)

F32 = mybir.dt.float32
BF16 = mybir.dt.bfloat16
I32 = mybir.dt.int32
U32 = mybir.dt.uint32
U16 = mybir.dt.uint16
U8 = mybir.dt.uint8
FP8X4 = mybir.dt.float8_e4m3fn_x4
FP4X4 = mybir.dt.float4_e2m1fn_x4
ALU = mybir.AluOpType
ACT = mybir.ActivationFunctionType

P = 128
PACK = 4
N = 512
R_PASSES = H // 512
HALVES = S // N
M_TILES = S2 // P
GPSIMD_SLICES = 2
RING_BANKS = 7


def tile_list_rope_window_scores_kernel(
    tc, tab_words, tab_scales, tab2_words, tab2_scales, w1, w4_words, w4_scales,
    b1, gain, tension, offs, offs2, pos1, pos2, out,
):
    nc = tc.nc
    with ExitStack() as ctx:
        keep = ctx.enter_context(tc.tile_pool(name="keep", bufs=1))
        ring = ctx.enter_context(tc.tile_pool(name="ring", bufs=2))
        psum = ctx.enter_context(tc.psum_pool(name="psum", bufs=1))
        taken = []

        def next_bank():
            taken.append(len(taken) % RING_BANKS)
            return psum.tile([P, N], F32, name="bank%d" % taken[-1])

        def held(name, shape, dtype, tag=None):
            return keep.tile(shape, dtype, name=name, tag=tag or name, align_bytes=64)

        offs_sb = held("offs_sb", [P, S // 16], U16)
        offs2_sb = held("offs2_sb", [P, S2 // 16], U16)
        pos1_sb = held("pos1_sb", [P, NP // 16], U16)
        pos2_sb = held("pos2_sb", [P, NP // 16], U16)

        w4w_raw = held("w4w_raw", [P, 2 * H], U8, tag="stage_a")
        w4s_raw = held("w4s_raw", [P, H], U8, tag="stage_b")
        tabw = held("tabw", [P, T], I32, tag="table_words")
        tabs = held("tabs", [P, T], U8, tag="stage_c")

        nc.vector.memset(tabs[:].bitcast(I32), 0)
        nc.gpsimd.memset(w4s_raw[:].bitcast(I32), 0)

        for tile, src in ((offs_sb, offs), (offs2_sb, offs2), (pos2_sb, pos2), (pos1_sb, pos1)):
            nc.sync.dma_start(tile[:], src)
        nc.sync.dma_start(w4w_raw[:].bitcast(I32), w4_words[0].bitcast(I32))
        nc.sync.dma_start(tabw[:], tab_words[0].rearrange("p t i -> p (t i)").bitcast(I32))
        nc.scalar.dma_start(tabs[0:P:8, :].bitcast(I32), tab_scales[0].bitcast(I32))
        for q in range(4):
            nc.scalar.dma_start(w4s_raw[32 * q : 32 * q + 4, :].bitcast(I32), w4_scales[0, 4 * q : 4 * q + 4, :].bitcast(I32))

        w4w = held("w4w", [P, 2 * H], U8)
        w4s = held("w4s", [P, H], U8)
        nc.vector.tensor_copy(
            w4w[:].bitcast(U16).rearrange("p (b t m) -> p b t m", b=R_PASSES, t=PACK),
            w4w_raw[:].bitcast(U16).rearrange("p (b m t) -> p b t m", b=R_PASSES, t=PACK),
        )
        vs_spread = held("vs_spread", [P, S], U8, tag="stage_d")
        nc.vector.tensor_copy(vs_spread[:], tabs[:].indirect(offs_sb[:]))
        nc.vector.tensor_copy(
            w4s[:].rearrange("p (b t m) -> p b t m", b=R_PASSES, t=PACK),
            w4s_raw[:].rearrange("p (b m t) -> p b t m", b=R_PASSES, t=PACK),
        )

        w1_rows = w1.rearrange("(p j) c -> p j c", j=PACK)
        w1_raw = [held("w1_raw%d" % b, [P, PACK, 512], F32, tag=("stage_a", "stage_b")[b]) for b in range(R_PASSES)]
        nc.sync.dma_start(w1_raw[0][:], w1_rows[:, :, 0:512])
        vs = held("vs", [P, S], U8)
        for q in range(4):
            nc.scalar.dma_start(vs[32 * q : 32 * q + 4, :].bitcast(I32), vs_spread[32 * q : 32 * (q + 1) : 8, :].bitcast(I32))
        nc.sync.dma_start(w1_raw[1][:], w1_rows[:, :, 512:1024])
        rows = held("rows", [P, 512], F32, tag="stage_c")
        nc.gpsimd.memset(rows[:], 0.0)
        nc.scalar.dma_start(rows[0:R_PASSES, :], b1.rearrange("(b c) -> b c", b=R_PASSES))
        nc.scalar.dma_start(rows[R_PASSES : 2 * R_PASSES, :], gain.rearrange("(b c) -> b c", b=R_PASSES))
        ident = held("ident", [P, P], F32)
        make_identity(nc, ident[:])

        vw = [held("vw%d" % u, [P, N], U32) for u in range(HALVES)]

        def gather_v(u):
            cols = offs_sb[:, u * N // 16 : (u + 1) * N // 16]
            nc.vector.tensor_copy(vw[u][:], tabw[:].bitcast(U32).indirect(cols))

        w1g = [held("w1g%d" % b, [P, 512 * PACK], BF16) for b in range(R_PASSES)]
        w1w = [held("w1w%d" % b, [P, 512], U32) for b in range(R_PASSES)]
        w1s = [held("w1s%d" % b, [P, 512], U8) for b in range(R_PASSES)]

        def weave_w1(b):
            nc.vector.tensor_copy(
                w1g[b][:].rearrange("p (t m j) -> p m j t", t=PACK, j=PACK),
                w1_raw[b][:].rearrange("p j (m t) -> p m j t", t=PACK),
            )

        def quant_w1(b):
            nc.vector.quantize_mx(out=w1w[b][:].bitcast(FP8X4), scales=w1s[b][:], in_=w1g[b][:])

        v2w = [held("v2w%d" % a, [P, S2], U32) for a in range(R_PASSES)]
        v2s = held("v2s", [P, S2], U8)

        def gather_v2():
            tab2w = held("tab2w", [P, R_PASSES * T3], I32, tag="table_words")
            tab2s = held("tab2s", [P, T3], U8, tag="stage_d")
            for a in range(R_PASSES):
                nc.sync.dma_start(tab2w[:, T3 * a : T3 * (a + 1)], tab2_words[a].rearrange("p t i -> p (t i)").bitcast(I32))
            nc.gpsimd.memset(tab2s[:].bitcast(I32), 0)
            for q in range(4):
                nc.sync.dma_start(tab2s[32 * q : 32 * q + 8, :].bitcast(I32), tab2_scales[:, 4 * q : 4 * q + 4, :].bitcast(I32))
            nc.vector.tensor_copy(v2s[:], tab2s[:].indirect(offs2_sb[:]))
            for a in range(R_PASSES):
                nc.vector.tensor_copy(v2w[a][:], tab2w[:, T3 * a : T3 * (a + 1)].bitcast(U32).indirect(offs2_sb[:]))

        chunks = [(u, b) for u in range(HALVES) for b in range(R_PASSES)]
        hw = [held("hw%d" % c, [P, N], U32) for c in range(len(chunks))]
        hs = [held("hs%d" % c, [P, N], U8) for c in range(len(chunks))]
        scores = [held("scores%d" % m, [P, S], F32) for m in range(M_TILES)]
        ga, gb, diff, hb, e_acc = {}, {}, {}, {}, {}

        def read_b(c, t):
            u, b = chunks[c]
            if t == 0:
                gb[c] = ring.tile([P, PACK, N], F32, name="gb", bufs=3)
            col = 512 * b + P * t
            acc = next_bank()
            nc.tensor.matmul_mx(
                out=acc[:], lhsT=w4w[:, 2 * col : 2 * (col + P)].bitcast(FP4X4), lhsT_scale=w4s[:, col : col + P],
                rhs=vw[u][:].bitcast(FP8X4), rhs_scale=vs[:, N * u : N * (u + 1)], start=True, stop=True,
            )
            nc.scalar.activation(gb[c][:, t, :], acc[:], ACT.Gelu_apprx_tanh)

        def read_a(c, t):
            u, b = chunks[c]
            if t == 0:
                ga[c] = ring.tile([P, PACK, N], F32, name="ga", bufs=3)
            acc = next_bank()
            nc.tensor.matmul_mx(
                out=acc[:], lhsT=w1w[b][:, P * t : P * (t + 1)].bitcast(FP8X4), lhsT_scale=w1s[b][:, P * t : P * (t + 1)],
                rhs=vw[u][:].bitcast(FP8X4), rhs_scale=vs[:, N * u : N * (u + 1)], start=True, stop=True,
            )
            nc.scalar.activation(ga[c][:, t, :], acc[:], ACT.Gelu_apprx_tanh, bias=b1_sb[:, t, b : b + 1])

        def read_both(c):
            for t in range(PACK):
                read_b(c, t)
                read_a(c, t)

        def subtract(c):
            diff[c] = ring.tile([P, PACK, N], F32, name="diff", bufs=3)
            for t in range(GPSIMD_SLICES):
                nc.gpsimd.tensor_tensor(diff[c][:, t, :], ga[c][:, t, :], gb[c][:, t, :], ALU.subtract)
            if c < len(chunks) - 1:
                rest = [slice(GPSIMD_SLICES, PACK)]
            else:
                rest = [slice(t, t + 1) for t in range(GPSIMD_SLICES, PACK)]
            for ts in rest:
                nc.vector.tensor_tensor(diff[c][:, ts, :], ga[c][:, ts, :], gb[c][:, ts, :], ALU.subtract)

        def scale_weave(c, j0, j1):
            u, b = chunks[c]
            if j0 == 0:
                hb[c] = ring.tile([P, N * PACK], BF16, name="hb", align_bytes=64)
            groups = (j1 - j0) // 2
            nc.vector.tensor_tensor(
                hb[c][:, PACK * j0 : PACK * j1].rearrange("p (g i t) -> p g t i", i=2, t=PACK),
                diff[c][:, :, j0:j1].rearrange("p t (g i) -> p g t i", i=2),
                turned[:, :, R_PASSES + b : R_PASSES + b + 1].rearrange("p (g t) i -> p g t i", g=1).to_broadcast([P, groups, PACK, 2]),
                ALU.mult,
            )

        def quant_h(c, j0, j1):
            nc.vector.quantize_mx(out=hw[c][:, j0:j1].bitcast(FP8X4), scales=hs[c][:, j0:j1], in_=hb[c][:, PACK * j0 : PACK * j1])

        def score(c, m):
            u, b = chunks[c]
            if b == 0:
                e_acc[m] = next_bank()
            nc.tensor.matmul_mx(
                out=e_acc[m][:], lhsT=v2w[b][:, P * m : P * (m + 1)].bitcast(FP8X4), lhsT_scale=v2s[4 * b : P, P * m : P * (m + 1)],
                rhs=hw[c][:].bitcast(FP8X4), rhs_scale=hs[c][:], start=(b == 0), stop=(b == R_PASSES - 1),
            )
            if b == R_PASSES - 1:
                nc.scalar.copy(scores[m][:, N * u : N * (u + 1)], e_acc[m][:])

        gather_v(0)
        for t in range(PACK):
            read_b(0, t)
        for t in range(PACK // 2):
            read_b(1, t)
        turned = psum.tile([P, PACK, P], F32, name="turned")
        for t in range(PACK):
            nc.tensor.transpose(turned[:, t, :], rows[:, t:512:PACK], ident[:])
        b1_sb = held("b1_sb", [P, PACK, R_PASSES], F32)
        nc.scalar.copy(b1_sb[:], turned[:, :, 0:R_PASSES])
        gather_v(1)
        weave_w1(0)
        quant_w1(0)
        for t in range(PACK):
            read_a(0, t)
        for t in range(PACK // 2, PACK):
            read_b(1, t)
        weave_w1(1)
        quant_w1(1)
        for t in range(PACK):
            read_a(1, t)
        subtract(0)
        scale_weave(0, 0, N)
        last = len(chunks) - 1
        for c in range(1, len(chunks)):
            if c + 1 <= last:
                read_both(c + 1)
            subtract(c)
            quant_h(c - 1, 0, N)
            if c == 1:
                gather_v2()
            if c < last:
                scale_weave(c, 0, N)
        for m in range(M_TILES):
            score(0, m)
            score(1, m)
        for m in range(M_TILES):
            score(2, m)
        scale_weave(last, 0, N // 2)
        scale_weave(last, N // 2, N)
        quant_h(last, 0, N // 2)
        quant_h(last, N // 2, N)
        for m in range(M_TILES):
            score(last, m)

        tens = held("tens", [P, M_TILES, NP], F32, tag="stage_a")
        nc.sync.dma_start(tens[:], tension.rearrange("(m p) j -> p m j", p=P))
        above, left = {}, {}

        def track(m):
            above[m] = ring.tile([P, NP], F32, name="above")
            left[m] = ring.tile([P, NP], F32, name="left")
            nc.vector.tensor_tensor(above[m][:], scores[m][:].indirect(pos2_sb[:]), tens[:, m, :], ALU.subtract)
            nc.scalar.mul(left[m][:], above[m][:], -1.0)

        def haul(m):
            res = ring.tile([P, NP], F32, name="res")
            width = NP if m < M_TILES - 1 else NP // 2
            for j in range(0, NP, width):
                picks = pos1_sb[:, j // 16 : (j + width) // 16]
                nc.vector.tensor_tensor(res[:, j : j + width], scores[m][:].indirect(picks), left[m][:, j : j + width], ALU.mult)
                nc.sync.dma_start(out[P * m : P * (m + 1), j : j + width], res[:, j : j + width])

        track(0)
        for m in range(M_TILES):
            if m + 1 < M_TILES:
                track(m + 1)
            haul(m)
